import numpy as np
import ml_dtypes


def mxq(x, axis, fmt="e4m3"):
    dtype, down = {"e4m3": (ml_dtypes.float8_e4m3fn, 7), "e5m2": (ml_dtypes.float8_e5m2, 14)}[fmt]
    v = np.moveaxis(np.asarray(x, np.float32).astype(ml_dtypes.bfloat16).astype(np.float64), axis, -1)
    blocks = v.reshape(v.shape[:-1] + (-1, 32))
    amax = np.abs(blocks).max(-1, keepdims=True)
    byte = np.maximum(np.where(amax > 0, np.frexp(amax)[1] - 1 + 127, 0) - down, 1)
    scale = np.exp2(byte - 127.0)
    codes = (blocks / scale).astype(np.float32).astype(dtype).astype(np.float64)
    return np.moveaxis((codes * scale).reshape(v.shape), -1, axis)


WIDE = False


def mx_kscale(k):
    if not WIDE:
        return np.ones(k)
    levels = np.array([10, -10, 5, -5, 0])
    if k % 512:
        return np.exp2(np.random.permutation(np.resize(levels, k // 32))).repeat(32)
    a = np.empty((k // 512, 16))
    for p in range(k // 512):
        a[p, :8] = np.random.permutation(np.resize(levels, 8))
        for g in range(8):
            far = levels[np.abs(levels - a[p, g]) >= 10]
            a[p, g + 8] = far[np.random.randint(len(far))]
    return np.exp2(a.ravel()).repeat(32)


def f64(x):
    return np.asarray(x).astype(np.float64)


def striped(idx):
    return np.tile(idx.reshape(-1, 16).T, (8, 1)).astype(np.uint16)


def unstriped(offs):
    return offs[:16].T.reshape(-1).astype(np.int64)


def striped8(idx):
    return np.concatenate([x.reshape(-1, 16).T for x in idx]).astype(np.uint16)


def runs(offs, k):
    lists = np.stack([offs[16 * r : 16 * r + 16].T.reshape(-1) for r in range(8)]).astype(np.int64)
    return lists[np.arange(k) % 512 // 64]


def pack_weight(w):
    k, n = w.shape
    w = f64(np.asarray(w, np.float32).astype(ml_dtypes.bfloat16)).reshape(k // 32, 32, n)
    amax = np.abs(w).max(1)
    byte = np.clip(np.where(amax > 0, np.frexp(amax)[1] - 1 + 127 - 7, 1), 1, 254)
    scaled = (w * np.exp2(127.0 - byte)[:, None, :]).reshape(k, n).astype(np.float32)
    words = np.ascontiguousarray(scaled.reshape(k // 512, 128, 4, n).transpose(0, 1, 3, 2)).astype(ml_dtypes.float8_e4m3fn).view(np.uint8)
    return words, np.ascontiguousarray(byte.astype(np.uint8).reshape(k // 512, 16, n))


def unpack_weight(words, scales):
    g, p, n, _ = words.shape
    vals = np.ascontiguousarray(words).view(ml_dtypes.float8_e4m3fn).astype(np.float64) * np.repeat(np.exp2(scales.astype(np.float64) - 127.0), 8, axis=1)[..., None]
    return vals.transpose(0, 1, 3, 2).reshape(g * 512, n)


K, T, S, N, G, H, W = 512, 1024, 512, 512, 2048, 512, 1024


def setup_inputs():
    n = np.random.standard_normal
    s = mx_kscale(K)[:, None]
    u = mx_kscale(S)
    packed_xT = pack_weight(n((K, T)) * s)
    packed_dT = pack_weight(n((K, G)) / s)
    return {
        "x_words": packed_xT[0],
        "x_scales": packed_xT[1],
        "d_words": packed_dT[0],
        "d_scales": packed_dT[1],
        "gn": (np.random.uniform(0.5, 1.5, (H, 1)) * u[:, None]).astype(np.float32),
        "w1": (n((H, N)) / np.sqrt(2 * H) / u[:, None]).astype(np.float32),
        "w2": (n((K, N)) / np.sqrt(2 * K) / s).astype(np.float32),
        "offs": striped(np.random.permutation(T)[:S]),
        "k1": striped8(np.random.randint(0, G, (8, H))),
        "n1": striped(np.random.randint(0, S, W)),
        "n2": striped(np.random.permutation(S)),
        "two": striped(np.random.permutation(T)[:S]),
        "n3": striped8(np.stack([np.random.permutation(S) for _ in range(8)])),
        "n4": striped8(np.stack([np.random.permutation(S) for _ in range(8)])),
    }


def reference(x_words, x_scales, d_words, d_scales, gn, w1, w2, offs, k1, n1, n2, two, n3, n4):
    d_k1 = unpack_weight(d_words, d_scales)[np.arange(K)[:, None], runs(k1, K)]
    xq = unpack_weight(x_words, x_scales)[:, unstriped(offs)]
    h = 0.0625 * (d_k1.T @ xq)
    mb = h[:, unstriped(n1)]
    mx = mb.reshape(H, S, 2).max(axis=2)
    st = h - mx
    z = f64(gn) * (np.maximum(st, st[:, unstriped(n2)]))
    x_two = unpack_weight(x_words, x_scales)[:, unstriped(two)]
    h2 = mxq(f64(w1), 0, "e4m3").T @ mxq(z, 0, "e4m3") + mxq(f64(w2), 0, "e4m3").T @ x_two
    st2 = np.maximum(h2, h2[np.arange(N)[:, None], runs(n3, N)])
    return st2[np.arange(N)[:, None], runs(n4, N)] - (0.5 * h2)

@@ -1,0 +1,253 @@
+from contextlib import ExitStack
+
+import concourse.mybir as mybir
+
+K, T, S, N, G, H, W = 512, 1024, 512, 512, 2048, 512, 1024
+FLOPS = 3 * 2 * 512 * 512 * 512
+
+F32 = mybir.dt.float32
+BF16 = mybir.dt.bfloat16
+I32 = mybir.dt.int32
+U32 = mybir.dt.uint32
+U16 = mybir.dt.uint16
+U8 = mybir.dt.uint8
+FP8X4 = mybir.dt.float8_e4m3fn_x4
+ALU = mybir.AluOpType
+ACT = mybir.ActivationFunctionType
+
+P = 128
+PACK = 4
+LIST_ROWS = 16
+SPARE = 16
+Z_CHUNKS = ((0, 128), (128, 256), (256, 384), (384, 512))
+HALF = S // 2
+
+
+def entries(list_tile, first, last):
+    return list_tile[:, first // LIST_ROWS : last // LIST_ROWS]
+
+
+def tile_picked_pqmixghopmhopb_none_p_kernel(tc, x_words, x_scales, d_words, d_scales, gn, w1, w2, offs, k1, n1, n2, two, n3, n4, out):
+    nc = tc.nc
+
+    with ExitStack() as ctx:
+        keep = ctx.enter_context(tc.tile_pool(name="keep", bufs=1))
+        psum = ctx.enter_context(tc.psum_pool(name="psum", bufs=1))
+
+        def load_list(name, dram):
+            list_tile = keep.tile(list(dram.shape), U16, name=name)
+            nc.sync.dma_start(list_tile[:], dram)
+            return list_tile
+
+        def gather(engine, dst, window, offsets):
+            if engine == "scalar":
+                nc.scalar.activation(dst, window.indirect(offsets), ACT.Copy)
+            else:
+                nc.vector.tensor_copy(dst, window.indirect(offsets))
+
+        d_scale_table = keep.tile([P, G], U8, align_bytes=64, tag="then_w2")
+        x_scale_table = keep.tile([P, T], U8, align_bytes=64)
+        d_scale_rows = keep.tile([P, H], U8, align_bytes=64, tag="then_x2_words")
+        nc.gpsimd.memset(x_scale_table[:].bitcast(I32), 0)
+        nc.vector.memset(d_scale_table[:].bitcast(I32), 0)
+        nc.vector.memset(d_scale_rows[:].bitcast(I32), 0)
+
+        k1_t = load_list("k1_t", k1)
+        nc.sync.dma_start(d_scale_table[0:P:8, :].bitcast(I32), d_scales[0].bitcast(I32))
+        x_table = keep.tile([P, T], I32, align_bytes=64)
+        nc.sync.dma_start(x_table[:], x_words[0].rearrange("p n r -> p (n r)").bitcast(I32))
+        offs_t = load_list("offs_t", offs)
+        for q, queue in enumerate((nc.scalar, nc.scalar, nc.scalar, nc.scalar)):
+            queue.dma_start(
+                x_scale_table[32 * q : 32 * q + 4, :].bitcast(I32), x_scales[0, 4 * q : 4 * q + 4, :].bitcast(I32)
+            )
+        d_table = keep.tile([P, G], I32, align_bytes=64)
+        nc.sync.dma_start(d_table[:], d_words[0].rearrange("p n r -> p (n r)").bitcast(I32))
+        two_t = load_list("two_t", two)
+        n1_t = load_list("n1_t", n1)
+        gn_t = keep.tile([P, PACK], F32)
+        nc.gpsimd.dma_start(gn_t[:], gn.rearrange("(p t) o -> p (t o)", t=PACK))
+
+        d_scale_picked = keep.tile([P, H], U8, align_bytes=64, tag="then_w1")
+        nc.vector.tensor_copy(d_scale_picked[:], d_scale_table[:].indirect(k1_t[:]))
+        for r, queue in enumerate((nc.scalar, nc.scalar, nc.sync, nc.sync)):
+            queue.dma_start(d_scale_rows[r:P:32, :].bitcast(I32), d_scale_picked[8 * r : P : 32, :].bitcast(I32))
+        w2_raw = keep.tile([P, PACK, N], F32, align_bytes=64, tag="then_w2")
+        nc.sync.dma_start(w2_raw[:], w2.rearrange("(p j) n -> p j n", j=PACK))
+        n2_t = load_list("n2_t", n2)
+        n3_t = load_list("n3_t", n3)
+        n4_t = load_list("n4_t", n4)
+
+        xq_words = keep.tile([P, S], U32, align_bytes=64, tag="x_picked_words")
+        nc.vector.tensor_copy(xq_words[:], x_table[:].bitcast(U32).indirect(offs_t[:]))
+        d_picked = keep.tile([P, H], U32, align_bytes=64, tag="then_scale_dealt")
+        nc.vector.tensor_copy(d_picked[:], d_table[:].bitcast(U32).indirect(k1_t[:]))
+        xq_scales = keep.tile([P, S], U8, align_bytes=64, tag="x_picked_scales")
+        nc.vector.tensor_copy(xq_scales[:], x_scale_table[:].indirect(offs_t[:]))
+        d_dealt = keep.tile([P, H], U32, align_bytes=64)
+        nc.vector.tensor_copy(
+            d_dealt[:].rearrange("p (t m) -> p m t", t=PACK),
+            d_picked[:].rearrange("p (m t) -> p m t", t=PACK),
+        )
+        d_scale_dealt = keep.tile([P, H], U8, align_bytes=64, tag="then_scale_dealt")
+        nc.vector.tensor_copy(
+            d_scale_dealt[:].rearrange("p (t m) -> p t m", t=PACK),
+            d_scale_rows[:].rearrange("p (m t) -> p t m", t=PACK),
+        )
+        w1_raw = keep.tile([P, PACK, N], F32, align_bytes=64, tag="then_w1")
+        nc.sync.dma_start(w1_raw[:], w1.rearrange("(p j) n -> p j n", j=PACK))
+
+        gain = keep.tile([P, PACK], F32)
+        nc.scalar.activation(gain[:], gn_t[:], ACT.Abs, scale=0.0625)
+        widest = max(b - a for a, b in Z_CHUNKS)
+        signs = keep.tile([P, widest, PACK], BF16, align_bytes=64)
+        nc.scalar.activation(signs[:], gn_t[:].unsqueeze(1).to_broadcast([P, widest, PACK]), ACT.Sign)
+
+        h_ps = []
+        for t in range(PACK):
+            bank = psum.tile([P, S], F32, name="h_ps%d" % t)
+            cols = slice(P * t, P * (t + 1))
+            nc.tensor.matmul_mx(
+                out=bank[:],
+                lhsT=d_dealt[:, cols].bitcast(FP8X4),
+                lhsT_scale=d_scale_dealt[:, cols],
+                rhs=xq_words[:].bitcast(FP8X4),
+                rhs_scale=xq_scales[:],
+                start=True,
+                stop=True,
+            )
+            h_ps.append(bank)
+
+        def round_weights(engine, raw, grouped, first, last):
+            dst = grouped[:].rearrange("p t m j -> p m j t")[:, first:last]
+            src = raw[:].rearrange("p j (m t) -> p m j t", t=PACK)[:, first:last]
+            if engine == "scalar":
+                nc.scalar.copy(dst, src)
+            elif engine == "gpsimd":
+                nc.gpsimd.tensor_copy(dst, src)
+            else:
+                nc.vector.tensor_copy(dst, src)
+
+        def quantize(name, grouped, width):
+            codes = keep.tile([P, width], U32, align_bytes=64, name=name + "_codes")
+            scales = keep.tile([P, width], U8, align_bytes=64, name=name + "_scales")
+            nc.vector.quantize_mx(out=codes[:].bitcast(FP8X4), scales=scales[:], in_=grouped)
+            return codes, scales
+
+        w2_grouped = keep.tile([P, PACK, P, PACK], BF16, align_bytes=64)
+        w1_grouped = keep.tile([P, PACK, P, PACK], BF16, align_bytes=64)
+
+        st = keep.tile([P, PACK, S], F32, align_bytes=64)
+        g1_engine = {key: "vector" for key in {(0, 1)}}
+
+        h_tiles = {}
+
+        def leave_psum(t):
+            h = keep.tile([P, S + SPARE], F32, name="h%d" % t)
+            nc.vector.memset(h[:, S:], 0.0)
+            nc.scalar.activation(h[:, :S], h_ps[t][:], ACT.Copy, scale=gain[:, t : t + 1])
+            h_tiles[t] = h
+
+        def less_larger_member(t, u):
+            h = h_tiles[t]
+            members = keep.tile([P, HALF, 2], F32, name="members%d_%d" % (t, u))
+            gather(
+                g1_engine.get((t, u), "scalar"),
+                members[:].rearrange("p j e -> p (j e)"),
+                h[:],
+                entries(n1_t, S * u, S * (u + 1)),
+            )
+            larger = keep.tile([P, HALF], F32, name="larger%d_%d" % (t, u))
+            nc.vector.tensor_tensor(larger[:], members[:, :, 0], members[:, :, 1], ALU.max)
+            cols = slice(HALF * u, HALF * (u + 1))
+            nc.vector.tensor_tensor(st[:, t, cols], h[:, cols], larger[:], ALU.subtract)
+
+        x2_words = keep.tile([P, S], U32, align_bytes=64, tag="then_x2_words")
+        nc.vector.tensor_copy(x2_words[:], x_table[:].bitcast(U32).indirect(two_t[:]))
+        leave_psum(0)
+        less_larger_member(0, 0)
+        less_larger_member(0, 1)
+        x2_scales = keep.tile([P, S], U8, align_bytes=64, tag="x_picked_scales")
+        nc.vector.tensor_copy(x2_scales[:], x_scale_table[:].indirect(two_t[:]))
+        leave_psum(1)
+        less_larger_member(1, 0)
+        less_larger_member(1, 1)
+        round_weights("vector", w2_raw, w2_grouped, 0, P)
+        leave_psum(2)
+        less_larger_member(2, 0)
+        w2_codes, w2_scales = quantize("w2", w2_grouped[:].rearrange("p t m j -> p (t m j)"), N)
+        round_weights("vector", w1_raw, w1_grouped, 0, P)
+        less_larger_member(2, 1)
+        leave_psum(3)
+        less_larger_member(3, 0)
+        w1_codes, w1_scales = quantize("w1", w1_grouped[:].rearrange("p t m j -> p (t m j)"), N)
+        less_larger_member(3, 1)
+
+        h2_ps = []
+        for t in range(PACK):
+            bank = psum.tile([P, S], F32, name="h2_ps%d" % t)
+            cols = slice(P * t, P * (t + 1))
+            nc.tensor.matmul_mx(
+                out=bank[:],
+                lhsT=w2_codes[:, cols].bitcast(FP8X4),
+                lhsT_scale=w2_scales[:, cols],
+                rhs=x2_words[:].bitcast(FP8X4),
+                rhs_scale=x2_scales[:],
+                start=True,
+                stop=False,
+            )
+            h2_ps.append(bank)
+
+        for first, last in Z_CHUNKS:
+            width = last - first
+            held = {128: "larger3_0", 256: "larger3_1", 384: "h3"}
+            st_n2 = keep.tile([P, PACK, width], F32, name="st_n2_%d" % first, tag=held.get(first, "st_n2"))
+            for t in range(PACK):
+                gather("vector" if (first, t) in {(0, 3)} else "scalar", st_n2[:, t, :], st[:, t, :], entries(n2_t, first, last))
+            z_abs = keep.tile([P, width, PACK], BF16, align_bytes=64, name="z_abs%d" % first, tag="z_abs", bufs=2)
+            nc.vector.tensor_tensor(
+                z_abs[:].rearrange("p (c i) t -> p c t i", i=4),
+                st[:, :, first:last].rearrange("p t (c i) -> p c t i", i=4),
+                st_n2[:].rearrange("p t (c i) -> p c t i", i=4),
+                ALU.max,
+            )
+            z = keep.tile([P, width, PACK], BF16, align_bytes=64, name="z%d" % first)
+            nc.vector.tensor_tensor(z[:], z_abs[:], signs[:, :width, :], ALU.mult)
+            z_codes, z_scales = quantize("z%d" % first, z[:].rearrange("p j t -> p (j t)"), width)
+            for t in range(PACK):
+                cols = slice(P * t, P * (t + 1))
+                nc.tensor.matmul_mx(
+                    out=h2_ps[t][:, first:last],
+                    lhsT=w1_codes[:, cols].bitcast(FP8X4),
+                    lhsT_scale=w1_scales[:, cols],
+                    rhs=z_codes[:].bitcast(FP8X4),
+                    rhs_scale=z_scales[:],
+                    start=False,
+                    stop=(last == S),
+                )
+
+        out_rows = out.rearrange("(p t) j -> t p j", t=PACK)
+        g3_engine = {key: "vector" for key in {(0,1),(1,1)}}
+        for t in range(PACK):
+            half_h2 = keep.tile([P, S], F32, name="half_h2_%d" % t)
+            if t in {1}:
+                nc.vector.tensor_scalar(half_h2[:], h2_ps[t][:], 0.5, None, ALU.mult)
+            else:
+                nc.scalar.activation(half_h2[:], h2_ps[t][:], ACT.Copy, scale=0.5)
+            st2 = keep.tile([P, S], F32, name="st2_%d" % t)
+            for u in range(2):
+                cols = slice(HALF * u, HALF * (u + 1))
+                half_n3 = keep.tile([P, HALF], F32, name="half_n3_%d_%d" % (t, u))
+                gather(g3_engine.get((t, u), "scalar"), half_n3[:], half_h2[:], entries(n3_t, cols.start, cols.stop))
+                nc.vector.scalar_tensor_tensor(st2[:, cols], half_n3[:], 2.0, h2_ps[t][:, cols], ALU.mult, ALU.max)
+            for u in range(2):
+                cols = slice(HALF * u, HALF * (u + 1))
+                result = keep.tile([P, HALF], F32, name="result%d_%d" % (t, u))
+                offsets = entries(n4_t, cols.start, cols.stop)
+                if (t, u) in {(3,1),(2,1),(1,1)}:
+                    st2_n4 = keep.tile([P, HALF], F32, name="st2_n4_%d_%d" % (t, u))
+                    gather("scalar", st2_n4[:], st2[:], offsets)
+                    nc.vector.tensor_tensor(result[:], st2_n4[:], half_h2[:, cols], ALU.subtract)
+                else:
+                    nc.vector.tensor_tensor(result[:], st2[:].indirect(offsets), half_h2[:, cols], ALU.subtract)
+                nc.sync.dma_start(out_rows[t][:, cols], result[:])

@@ -47,55 +47,63 @@ def tile_picked_pqmixghopmhopb_none_p_kernel(tc, x_words, x_scales, d_words, d_s
 
         d_scale_table = keep.tile([P, G], U8, align_bytes=64, tag="then_w2")
         x_scale_table = keep.tile([P, T], U8, align_bytes=64)
-        d_scale_rows = keep.tile([P, H], U8, align_bytes=64, tag="then_x2_words")
-        nc.gpsimd.memset(x_scale_table[:].bitcast(I32), 0)
-        nc.vector.memset(d_scale_table[:].bitcast(I32), 0)
+        d_scale_rows = keep.tile([P, H], U8, align_bytes=64, tag="then_d_dealt")
+        nc.gpsimd.memset(d_scale_table[:].bitcast(I32), 0)
+        nc.vector.memset(x_scale_table[:].bitcast(I32), 0)
         nc.vector.memset(d_scale_rows[:].bitcast(I32), 0)
 
         k1_t = load_list("k1_t", k1)
-        nc.sync.dma_start(d_scale_table[0:P:8, :].bitcast(I32), d_scales[0].bitcast(I32))
-        x_table = keep.tile([P, T], I32, align_bytes=64)
-        nc.sync.dma_start(x_table[:], x_words[0].rearrange("p n r -> p (n r)").bitcast(I32))
         offs_t = load_list("offs_t", offs)
-        for q, queue in enumerate((nc.scalar, nc.scalar, nc.scalar, nc.scalar)):
+        nc.sync.dma_start(d_scale_table[0:P:8, :].bitcast(I32), d_scales[0].bitcast(I32))
+        for q, queue in enumerate((nc.scalar, nc.scalar, nc.scalar, nc.sync)):
             queue.dma_start(
                 x_scale_table[32 * q : 32 * q + 4, :].bitcast(I32), x_scales[0, 4 * q : 4 * q + 4, :].bitcast(I32)
             )
         d_table = keep.tile([P, G], I32, align_bytes=64)
         nc.sync.dma_start(d_table[:], d_words[0].rearrange("p n r -> p (n r)").bitcast(I32))
-        two_t = load_list("two_t", two)
+        x_table = keep.tile([P, T], I32, align_bytes=64)
+        nc.sync.dma_start(x_table[:], x_words[0].rearrange("p n r -> p (n r)").bitcast(I32))
         n1_t = load_list("n1_t", n1)
         gn_t = keep.tile([P, PACK], F32)
-        nc.gpsimd.dma_start(gn_t[:], gn.rearrange("(p t) o -> p (t o)", t=PACK))
+        nc.sync.dma_start(gn_t[:], gn.rearrange("(p t) o -> p (t o)", t=PACK))
 
         d_scale_picked = keep.tile([P, H], U8, align_bytes=64, tag="then_w1")
         nc.vector.tensor_copy(d_scale_picked[:], d_scale_table[:].indirect(k1_t[:]))
         for r, queue in enumerate((nc.scalar, nc.scalar, nc.sync, nc.sync)):
             queue.dma_start(d_scale_rows[r:P:32, :].bitcast(I32), d_scale_picked[8 * r : P : 32, :].bitcast(I32))
+        two_t = load_list("two_t", two)
         w2_raw = keep.tile([P, PACK, N], F32, align_bytes=64, tag="then_w2")
         nc.sync.dma_start(w2_raw[:], w2.rearrange("(p j) n -> p j n", j=PACK))
         n2_t = load_list("n2_t", n2)
         n3_t = load_list("n3_t", n3)
         n4_t = load_list("n4_t", n4)
+        w1_raw = keep.tile([P, PACK, N], F32, align_bytes=64, tag="then_w1")
+        nc.sync.dma_start(w1_raw[:], w1.rearrange("(p j) n -> p j n", j=PACK))
 
-        xq_words = keep.tile([P, S], U32, align_bytes=64, tag="x_picked_words")
-        nc.vector.tensor_copy(xq_words[:], x_table[:].bitcast(U32).indirect(offs_t[:]))
-        d_picked = keep.tile([P, H], U32, align_bytes=64, tag="then_scale_dealt")
-        nc.vector.tensor_copy(d_picked[:], d_table[:].bitcast(U32).indirect(k1_t[:]))
         xq_scales = keep.tile([P, S], U8, align_bytes=64, tag="x_picked_scales")
         nc.vector.tensor_copy(xq_scales[:], x_scale_table[:].indirect(offs_t[:]))
-        d_dealt = keep.tile([P, H], U32, align_bytes=64)
-        nc.vector.tensor_copy(
-            d_dealt[:].rearrange("p (t m) -> p m t", t=PACK),
-            d_picked[:].rearrange("p (m t) -> p m t", t=PACK),
-        )
-        d_scale_dealt = keep.tile([P, H], U8, align_bytes=64, tag="then_scale_dealt")
+        d_picked = []
+        for u, tag in enumerate(("then_xq_words", "then_x2_words")):
+            words = keep.tile([P, HALF], U32, align_bytes=64, name="d_picked%d" % u, tag=tag)
+            nc.vector.tensor_copy(words[:], d_table[:].bitcast(U32).indirect(entries(k1_t, HALF * u, HALF * (u + 1))))
+            d_picked.append(words)
+        d_scale_dealt = keep.tile([P, H], U8, align_bytes=64)
         nc.vector.tensor_copy(
             d_scale_dealt[:].rearrange("p (t m) -> p t m", t=PACK),
             d_scale_rows[:].rearrange("p (m t) -> p t m", t=PACK),
         )
-        w1_raw = keep.tile([P, PACK, N], F32, align_bytes=64, tag="then_w1")
-        nc.sync.dma_start(w1_raw[:], w1.rearrange("(p j) n -> p j n", j=PACK))
+        d_dealt = keep.tile([P, PACK, P], U32, align_bytes=64, tag="then_d_dealt")
+        for u in range(2):
+            nc.vector.tensor_copy(
+                d_dealt[:, :, P // 2 * u : P // 2 * (u + 1)].rearrange("p t m -> p m t"),
+                d_picked[u][:].rearrange("p (m t) -> p m t", t=PACK),
+            )
+        xq_words = keep.tile([P, S], U32, align_bytes=64, tag="then_xq_words")
+        for u in range(2):
+            nc.vector.tensor_copy(
+                xq_words[:, HALF * u : HALF * (u + 1)],
+                x_table[:].bitcast(U32).indirect(entries(offs_t, HALF * u, HALF * (u + 1))),
+            )
 
         gain = keep.tile([P, PACK], F32)
         nc.scalar.activation(gain[:], gn_t[:], ACT.Abs, scale=0.0625)
@@ -105,28 +113,30 @@ def tile_picked_pqmixghopmhopb_none_p_kernel(tc, x_words, x_scales, d_words, d_s
 
         h_ps = []
         for t in range(PACK):
-            bank = psum.tile([P, S], F32, name="h_ps%d" % t)
-            cols = slice(P * t, P * (t + 1))
-            nc.tensor.matmul_mx(
-                out=bank[:],
-                lhsT=d_dealt[:, cols].bitcast(FP8X4),
-                lhsT_scale=d_scale_dealt[:, cols],
-                rhs=xq_words[:].bitcast(FP8X4),
-                rhs_scale=xq_scales[:],
-                start=True,
-                stop=True,
-            )
-            h_ps.append(bank)
+            pieces = []
+            for first, last in ((0, HALF), (HALF, S)) if t == 0 else ((0, S),):
+                bank = psum.tile([P, last - first], F32, name="h_ps%d_%d" % (t, first))
+                nc.tensor.matmul_mx(
+                    out=bank[:],
+                    lhsT=d_dealt[:, t, :].bitcast(FP8X4),
+                    lhsT_scale=d_scale_dealt[:, P * t : P * (t + 1)],
+                    rhs=xq_words[:, first:last].bitcast(FP8X4),
+                    rhs_scale=xq_scales[:, first:last],
+                    start=True,
+                    stop=True,
+                )
+                pieces.append((first, last, bank))
+            h_ps.append(pieces)
 
-        def round_weights(engine, raw, grouped, first, last):
-            dst = grouped[:].rearrange("p t m j -> p m j t")[:, first:last]
-            src = raw[:].rearrange("p j (m t) -> p m j t", t=PACK)[:, first:last]
+        def round_weights(engine, raw, pair, tag):
+            grouped = keep.tile([P, 2, P, PACK], BF16, align_bytes=64, name="grouped_%s%d" % (tag, pair), tag=tag)
+            dst = grouped[:].rearrange("p t m j -> p m j t")
+            src = raw[:].rearrange("p j (m t) -> p m j t", t=PACK)[:, :, :, 2 * pair : 2 * pair + 2]
             if engine == "scalar":
                 nc.scalar.copy(dst, src)
-            elif engine == "gpsimd":
-                nc.gpsimd.tensor_copy(dst, src)
             else:
                 nc.vector.tensor_copy(dst, src)
+            return grouped[:].rearrange("p t m j -> p (t m j)")
 
         def quantize(name, grouped, width):
             codes = keep.tile([P, width], U32, align_bytes=64, name=name + "_codes")
@@ -134,30 +144,26 @@ def tile_picked_pqmixghopmhopb_none_p_kernel(tc, x_words, x_scales, d_words, d_s
             nc.vector.quantize_mx(out=codes[:].bitcast(FP8X4), scales=scales[:], in_=grouped)
             return codes, scales
 
-        w2_grouped = keep.tile([P, PACK, P, PACK], BF16, align_bytes=64)
-        w1_grouped = keep.tile([P, PACK, P, PACK], BF16, align_bytes=64)
-
         st = keep.tile([P, PACK, S], F32, align_bytes=64)
-        g1_engine = {key: "vector" for key in {(0, 1)}}
-
         h_tiles = {}
 
         def leave_psum(t):
-            h = keep.tile([P, S + SPARE], F32, name="h%d" % t)
+            h = keep.tile([P, S + SPARE], F32, align_bytes=64, name="h%d" % t)
             nc.vector.memset(h[:, S:], 0.0)
-            nc.scalar.activation(h[:, :S], h_ps[t][:], ACT.Copy, scale=gain[:, t : t + 1])
+            for first, last, bank in h_ps[t]:
+                nc.scalar.activation(h[:, first:last], bank[:], ACT.Copy, scale=gain[:, t : t + 1])
             h_tiles[t] = h
 
         def less_larger_member(t, u):
             h = h_tiles[t]
-            members = keep.tile([P, HALF, 2], F32, name="members%d_%d" % (t, u))
+            members = keep.tile([P, HALF, 2], F32, align_bytes=64, name="members%d_%d" % (t, u))
             gather(
-                g1_engine.get((t, u), "scalar"),
+                "vector" if (t, u) in {(0, 1), (1, 1)} else "scalar",
                 members[:].rearrange("p j e -> p (j e)"),
                 h[:],
                 entries(n1_t, S * u, S * (u + 1)),
             )
-            larger = keep.tile([P, HALF], F32, name="larger%d_%d" % (t, u))
+            larger = keep.tile([P, HALF], F32, align_bytes=64, name="larger%d_%d" % (t, u))
             nc.vector.tensor_tensor(larger[:], members[:, :, 0], members[:, :, 1], ALU.max)
             cols = slice(HALF * u, HALF * (u + 1))
             nc.vector.tensor_tensor(st[:, t, cols], h[:, cols], larger[:], ALU.subtract)
@@ -172,79 +178,103 @@ def tile_picked_pqmixghopmhopb_none_p_kernel(tc, x_words, x_scales, d_words, d_s
         leave_psum(1)
         less_larger_member(1, 0)
         less_larger_member(1, 1)
-        round_weights("vector", w2_raw, w2_grouped, 0, P)
+        w2_early = round_weights("vector", w2_raw, 0, "w2_early")
         leave_psum(2)
         less_larger_member(2, 0)
-        w2_codes, w2_scales = quantize("w2", w2_grouped[:].rearrange("p t m j -> p (t m j)"), N)
-        round_weights("vector", w1_raw, w1_grouped, 0, P)
+        w2_mx = [quantize("w2_early", w2_early, HALF)]
+        w1_early = round_weights("vector", w1_raw, 0, "w1_early")
         less_larger_member(2, 1)
         leave_psum(3)
         less_larger_member(3, 0)
-        w1_codes, w1_scales = quantize("w1", w1_grouped[:].rearrange("p t m j -> p (t m j)"), N)
+        w1_mx = [quantize("w1_early", w1_early, HALF)]
         less_larger_member(3, 1)
 
-        h2_ps = []
-        for t in range(PACK):
-            bank = psum.tile([P, S], F32, name="h2_ps%d" % t)
-            cols = slice(P * t, P * (t + 1))
-            nc.tensor.matmul_mx(
-                out=bank[:],
-                lhsT=w2_codes[:, cols].bitcast(FP8X4),
-                lhsT_scale=w2_scales[:, cols],
-                rhs=x2_words[:].bitcast(FP8X4),
-                rhs_scale=x2_scales[:],
-                start=True,
-                stop=False,
-            )
-            h2_ps.append(bank)
+        h2_ps = {}
+        for t, tags in enumerate((("h_ps0_0", "h_ps0_256"), ("h_ps1_0", "h2_ps1"), ("h2_ps2",), ("h2_ps3",))):
+            width = S // len(tags)
+            for u, tag in enumerate(tags):
+                h2_ps[t, width * u] = psum.tile([P, width], F32, name="h2_ps%d_%d" % (t, u), tag=tag)
 
+        def h2_view(t, first, last):
+            base = first // HALF * HALF if t < 2 else 0
+            return h2_ps[t, base][:, first - base : last - base]
+
+        def product(t, weights, moving, first, last, start, stop):
+            codes, scales = weights[t // 2]
+            cols = slice(P * (t % 2), P * (t % 2 + 1))
+            nc.tensor.matmul_mx(
+                out=h2_view(t, first, last),
+                lhsT=codes[:, cols].bitcast(FP8X4),
+                lhsT_scale=scales[:, cols],
+                rhs=moving[0][:, first:last].bitcast(FP8X4),
+                rhs_scale=moving[1][:, first:last],
+                start=start,
+                stop=stop,
+            )
+
+        for t in range(2):
+            for first in (0, HALF):
+                product(t, w2_mx, (x2_words, x2_scales), first, first + HALF, True, False)
+
+        held = {128: "larger3_0", 256: "larger3_1", 384: "h3"}
+        st_n2 = {}
+        for first, last in Z_CHUNKS:
+            st_n2[first] = keep.tile(
+                [P, PACK, last - first], F32, align_bytes=64, name="st_n2_%d" % first, tag=held.get(first, "st_n2")
+            )
+            for t in range(PACK):
+                gather("vector" if (first, t) in {(0, 2), (0, 3), (128, 3)} else "scalar", st_n2[first][:, t, :], st[:, t, :], entries(n2_t, first, last))
+        z_codes = keep.tile([P, S], U32, align_bytes=64)
+        z_scales = keep.tile([P, S], U8, align_bytes=64)
         for first, last in Z_CHUNKS:
             width = last - first
-            held = {128: "larger3_0", 256: "larger3_1", 384: "h3"}
-            st_n2 = keep.tile([P, PACK, width], F32, name="st_n2_%d" % first, tag=held.get(first, "st_n2"))
-            for t in range(PACK):
-                gather("vector" if (first, t) in {(0, 3)} else "scalar", st_n2[:, t, :], st[:, t, :], entries(n2_t, first, last))
             z_abs = keep.tile([P, width, PACK], BF16, align_bytes=64, name="z_abs%d" % first, tag="z_abs", bufs=2)
             nc.vector.tensor_tensor(
                 z_abs[:].rearrange("p (c i) t -> p c t i", i=4),
                 st[:, :, first:last].rearrange("p t (c i) -> p c t i", i=4),
-                st_n2[:].rearrange("p t (c i) -> p c t i", i=4),
+                st_n2[first][:].rearrange("p t (c i) -> p c t i", i=4),
                 ALU.max,
             )
             z = keep.tile([P, width, PACK], BF16, align_bytes=64, name="z%d" % first)
             nc.vector.tensor_tensor(z[:], z_abs[:], signs[:, :width, :], ALU.mult)
-            z_codes, z_scales = quantize("z%d" % first, z[:].rearrange("p j t -> p (j t)"), width)
-            for t in range(PACK):
-                cols = slice(P * t, P * (t + 1))
-                nc.tensor.matmul_mx(
-                    out=h2_ps[t][:, first:last],
-                    lhsT=w1_codes[:, cols].bitcast(FP8X4),
-                    lhsT_scale=w1_scales[:, cols],
-                    rhs=z_codes[:].bitcast(FP8X4),
-                    rhs_scale=z_scales[:],
-                    start=False,
-                    stop=(last == S),
-                )
+            nc.vector.quantize_mx(
+                out=z_codes[:, first:last].bitcast(FP8X4),
+                scales=z_scales[:, first:last],
+                in_=z[:].rearrange("p j t -> p (j t)"),
+            )
+            for t in range(2):
+                product(t, w1_mx, (z_codes, z_scales), first, last, False, last % HALF == 0)
+
+        w1_mx.append(quantize("w1_late", round_weights("scalar", w1_raw, 1, "st_n2"), HALF))
+        w2_mx.append(quantize("w2_late", round_weights("scalar", w2_raw, 1, "larger3_0"), HALF))
+        for t in range(2, PACK):
+            product(t, w1_mx, (z_codes, z_scales), 0, S, True, False)
+            product(t, w2_mx, (x2_words, x2_scales), 0, S, False, True)
 
         out_rows = out.rearrange("(p t) j -> t p j", t=PACK)
-        g3_engine = {key: "vector" for key in {(0,1),(1,1)}}
+        half_h2s, st2s = [], []
         for t in range(PACK):
             half_h2 = keep.tile([P, S], F32, name="half_h2_%d" % t)
-            if t in {1}:
-                nc.vector.tensor_scalar(half_h2[:], h2_ps[t][:], 0.5, None, ALU.mult)
-            else:
-                nc.scalar.activation(half_h2[:], h2_ps[t][:], ACT.Copy, scale=0.5)
+            for first, last in ((0, HALF), (HALF, S)) if t < 2 else ((0, S),):
+                if (t, first) in {(1, 256)}:
+                    nc.vector.tensor_scalar(half_h2[:, first:last], h2_view(t, first, last), 0.5, None, ALU.mult)
+                else:
+                    nc.scalar.activation(half_h2[:, first:last], h2_view(t, first, last), ACT.Copy, scale=0.5)
             st2 = keep.tile([P, S], F32, name="st2_%d" % t)
             for u in range(2):
                 cols = slice(HALF * u, HALF * (u + 1))
                 half_n3 = keep.tile([P, HALF], F32, name="half_n3_%d_%d" % (t, u))
-                gather(g3_engine.get((t, u), "scalar"), half_n3[:], half_h2[:], entries(n3_t, cols.start, cols.stop))
-                nc.vector.scalar_tensor_tensor(st2[:, cols], half_n3[:], 2.0, h2_ps[t][:, cols], ALU.mult, ALU.max)
+                gather("vector" if (t, u) in {(0, 1), (1, 1)} else "scalar", half_n3[:], half_h2[:], entries(n3_t, cols.start, cols.stop))
+                nc.vector.scalar_tensor_tensor(st2[:, cols], half_n3[:], 2.0, h2_view(t, cols.start, cols.stop), ALU.mult, ALU.max)
+            half_h2s.append(half_h2)
+            st2s.append(st2)
+        for t in range(PACK):
+            half_h2, st2 = half_h2s[t], st2s[t]
             for u in range(2):
                 cols = slice(HALF * u, HALF * (u + 1))
                 result = keep.tile([P, HALF], F32, name="result%d_%d" % (t, u))
                 offsets = entries(n4_t, cols.start, cols.stop)
-                if (t, u) in {(3,1),(2,1),(1,1)}:
+                if (t, u) in {(1, 1), (2, 1), (3, 0), (3, 1)}:
                     st2_n4 = keep.tile([P, HALF], F32, name="st2_n4_%d_%d" % (t, u))
                     gather("scalar", st2_n4[:], st2[:], offsets)
                     nc.vector.tensor_tensor(result[:], st2_n4[:], half_h2[:, cols], ALU.subtract)

@@ -47,15 +47,15 @@ def tile_picked_pqmixghopmhopb_none_p_kernel(tc, x_words, x_scales, d_words, d_s
 
         d_scale_table = keep.tile([P, G], U8, align_bytes=64, tag="then_w2")
         x_scale_table = keep.tile([P, T], U8, align_bytes=64)
-        d_scale_rows = keep.tile([P, H], U8, align_bytes=64, tag="then_d_dealt")
-        nc.gpsimd.memset(d_scale_table[:].bitcast(I32), 0)
+        d_scale_rows = keep.tile([P, H], U8, align_bytes=64, tag="then_x2_words")
+        nc.vector.memset(d_scale_table[:].bitcast(I32), 0)
         nc.vector.memset(x_scale_table[:].bitcast(I32), 0)
         nc.vector.memset(d_scale_rows[:].bitcast(I32), 0)
 
         k1_t = load_list("k1_t", k1)
         offs_t = load_list("offs_t", offs)
         nc.sync.dma_start(d_scale_table[0:P:8, :].bitcast(I32), d_scales[0].bitcast(I32))
-        for q, queue in enumerate((nc.scalar, nc.scalar, nc.scalar, nc.sync)):
+        for q, queue in enumerate((nc.scalar, nc.scalar, nc.sync, nc.sync)):
             queue.dma_start(
                 x_scale_table[32 * q : 32 * q + 4, :].bitcast(I32), x_scales[0, 4 * q : 4 * q + 4, :].bitcast(I32)
             )
@@ -63,47 +63,51 @@ def tile_picked_pqmixghopmhopb_none_p_kernel(tc, x_words, x_scales, d_words, d_s
         nc.sync.dma_start(d_table[:], d_words[0].rearrange("p n r -> p (n r)").bitcast(I32))
         x_table = keep.tile([P, T], I32, align_bytes=64)
         nc.sync.dma_start(x_table[:], x_words[0].rearrange("p n r -> p (n r)").bitcast(I32))
-        n1_t = load_list("n1_t", n1)
         gn_t = keep.tile([P, PACK], F32)
         nc.sync.dma_start(gn_t[:], gn.rearrange("(p t) o -> p (t o)", t=PACK))
 
-        d_scale_picked = keep.tile([P, H], U8, align_bytes=64, tag="then_w1")
+        d_scale_picked = keep.tile([P, H], U8, align_bytes=64, tag="then_xq1")
         nc.vector.tensor_copy(d_scale_picked[:], d_scale_table[:].indirect(k1_t[:]))
-        for r, queue in enumerate((nc.scalar, nc.scalar, nc.sync, nc.sync)):
-            queue.dma_start(d_scale_rows[r:P:32, :].bitcast(I32), d_scale_picked[8 * r : P : 32, :].bitcast(I32))
+        for r in range(4):
+            nc.sync.dma_start(d_scale_rows[r:P:32, :].bitcast(I32), d_scale_picked[8 * r : P : 32, :].bitcast(I32))
+        n1_t = load_list("n1_t", n1)
         two_t = load_list("two_t", two)
         w2_raw = keep.tile([P, PACK, N], F32, align_bytes=64, tag="then_w2")
         nc.sync.dma_start(w2_raw[:], w2.rearrange("(p j) n -> p j n", j=PACK))
-        n2_t = load_list("n2_t", n2)
-        n3_t = load_list("n3_t", n3)
-        n4_t = load_list("n4_t", n4)
-        w1_raw = keep.tile([P, PACK, N], F32, align_bytes=64, tag="then_w1")
-        nc.sync.dma_start(w1_raw[:], w1.rearrange("(p j) n -> p j n", j=PACK))
 
         xq_scales = keep.tile([P, S], U8, align_bytes=64, tag="x_picked_scales")
         nc.vector.tensor_copy(xq_scales[:], x_scale_table[:].indirect(offs_t[:]))
         d_picked = []
-        for u, tag in enumerate(("then_xq_words", "then_x2_words")):
+        for u, tag in enumerate(("then_xq0", "then_w1")):
             words = keep.tile([P, HALF], U32, align_bytes=64, name="d_picked%d" % u, tag=tag)
             nc.vector.tensor_copy(words[:], d_table[:].bitcast(U32).indirect(entries(k1_t, HALF * u, HALF * (u + 1))))
             d_picked.append(words)
-        d_scale_dealt = keep.tile([P, H], U8, align_bytes=64)
-        nc.vector.tensor_copy(
-            d_scale_dealt[:].rearrange("p (t m) -> p t m", t=PACK),
-            d_scale_rows[:].rearrange("p (m t) -> p t m", t=PACK),
-        )
-        d_dealt = keep.tile([P, PACK, P], U32, align_bytes=64, tag="then_d_dealt")
+        d_dealt = keep.tile([P, PACK, P], U32, align_bytes=64)
         for u in range(2):
             nc.vector.tensor_copy(
                 d_dealt[:, :, P // 2 * u : P // 2 * (u + 1)].rearrange("p t m -> p m t"),
                 d_picked[u][:].rearrange("p (m t) -> p m t", t=PACK),
             )
-        xq_words = keep.tile([P, S], U32, align_bytes=64, tag="then_xq_words")
-        for u in range(2):
-            nc.vector.tensor_copy(
-                xq_words[:, HALF * u : HALF * (u + 1)],
-                x_table[:].bitcast(U32).indirect(entries(offs_t, HALF * u, HALF * (u + 1))),
-            )
+        xq_words = []
+
+        def pick_x_words(u):
+            words = keep.tile([P, HALF], U32, align_bytes=64, name="xq_words%d" % u, tag="then_xq%d" % u)
+            nc.vector.tensor_copy(words[:], x_table[:].bitcast(U32).indirect(entries(offs_t, HALF * u, HALF * (u + 1))))
+            xq_words.append(words)
+
+        pick_x_words(0)
+        d_scale_dealt = keep.tile([P, H], U8, align_bytes=64)
+        nc.vector.tensor_copy(
+            d_scale_dealt[:].rearrange("p (t m) -> p t m", t=PACK),
+            d_scale_rows[:].rearrange("p (m t) -> p t m", t=PACK),
+        )
+        pick_x_words(1)
+        w1_raw = keep.tile([P, PACK, N], F32, align_bytes=64, tag="then_w1")
+        nc.sync.dma_start(w1_raw[:], w1.rearrange("(p j) n -> p j n", j=PACK))
+
+        n2_t = load_list("n2_t", n2)
+        n3_t = load_list("n3_t", n3)
+        n4_t = load_list("n4_t", n4)
 
         gain = keep.tile([P, PACK], F32)
         nc.scalar.activation(gain[:], gn_t[:], ACT.Abs, scale=0.0625)
@@ -113,19 +117,24 @@ def tile_picked_pqmixghopmhopb_none_p_kernel(tc, x_words, x_scales, d_words, d_s
 
         h_ps = []
         for t in range(PACK):
-            pieces = []
-            for first, last in ((0, HALF), (HALF, S)) if t == 0 else ((0, S),):
-                bank = psum.tile([P, last - first], F32, name="h_ps%d_%d" % (t, first))
+            if t < 2:
+                banks = [psum.tile([P, HALF], F32, name="h_ps%d_%d" % (t, HALF * u)) for u in range(2)]
+                pieces = [(HALF * u, HALF * (u + 1), banks[u]) for u in range(2)]
+                halves = [bank[:] for bank in banks]
+            else:
+                bank = psum.tile([P, S], F32, name="h_ps%d_0" % t)
+                pieces = [(0, S, bank)]
+                halves = [bank[:, :HALF], bank[:, HALF:]]
+            for u in range(2):
                 nc.tensor.matmul_mx(
-                    out=bank[:],
+                    out=halves[u],
                     lhsT=d_dealt[:, t, :].bitcast(FP8X4),
                     lhsT_scale=d_scale_dealt[:, P * t : P * (t + 1)],
-                    rhs=xq_words[:, first:last].bitcast(FP8X4),
-                    rhs_scale=xq_scales[:, first:last],
+                    rhs=xq_words[u][:].bitcast(FP8X4),
+                    rhs_scale=xq_scales[:, HALF * u : HALF * (u + 1)],
                     start=True,
                     stop=True,
                 )
-                pieces.append((first, last, bank))
             h_ps.append(pieces)
 
         def round_weights(engine, raw, pair, tag):
@@ -156,28 +165,29 @@ def tile_picked_pqmixghopmhopb_none_p_kernel(tc, x_words, x_scales, d_words, d_s
 
         def less_larger_member(t, u):
             h = h_tiles[t]
-            members = keep.tile([P, HALF, 2], F32, align_bytes=64, name="members%d_%d" % (t, u))
-            gather(
-                "vector" if (t, u) in {(0, 1), (1, 1)} else "scalar",
-                members[:].rearrange("p j e -> p (j e)"),
-                h[:],
-                entries(n1_t, S * u, S * (u + 1)),
-            )
-            larger = keep.tile([P, HALF], F32, align_bytes=64, name="larger%d_%d" % (t, u))
+            halves = (0, 1) if t < 2 else (u,)
+            width = HALF * len(halves)
+            members = keep.tile([P, width, 2], F32, align_bytes=64, name="members%d_%d" % (t, u))
+            for v in halves:
+                gather(
+                    "vector" if t < 2 and v == 1 else "scalar",
+                    members[:, HALF * (v - u) : HALF * (v - u + 1), :].rearrange("p j e -> p (j e)"),
+                    h[:],
+                    entries(n1_t, S * v, S * (v + 1)),
+                )
+            larger = keep.tile([P, width], F32, align_bytes=64, name="larger%d_%d" % (t, u))
             nc.vector.tensor_tensor(larger[:], members[:, :, 0], members[:, :, 1], ALU.max)
-            cols = slice(HALF * u, HALF * (u + 1))
+            cols = slice(HALF * u, HALF * u + width)
             nc.vector.tensor_tensor(st[:, t, cols], h[:, cols], larger[:], ALU.subtract)
 
         x2_words = keep.tile([P, S], U32, align_bytes=64, tag="then_x2_words")
         nc.vector.tensor_copy(x2_words[:], x_table[:].bitcast(U32).indirect(two_t[:]))
         leave_psum(0)
         less_larger_member(0, 0)
-        less_larger_member(0, 1)
         x2_scales = keep.tile([P, S], U8, align_bytes=64, tag="x_picked_scales")
         nc.vector.tensor_copy(x2_scales[:], x_scale_table[:].indirect(two_t[:]))
         leave_psum(1)
         less_larger_member(1, 0)
-        less_larger_member(1, 1)
         w2_early = round_weights("vector", w2_raw, 0, "w2_early")
         leave_psum(2)
         less_larger_member(2, 0)
@@ -190,7 +200,7 @@ def tile_picked_pqmixghopmhopb_none_p_kernel(tc, x_words, x_scales, d_words, d_s
         less_larger_member(3, 1)
 
         h2_ps = {}
-        for t, tags in enumerate((("h_ps0_0", "h_ps0_256"), ("h_ps1_0", "h2_ps1"), ("h2_ps2",), ("h2_ps3",))):
+        for t, tags in enumerate((("h_ps0_0", "h_ps0_256"), ("h_ps1_0", "h_ps1_256"), ("h2_ps2",), ("h2_ps3",))):
             width = S // len(tags)
             for u, tag in enumerate(tags):
                 h2_ps[t, width * u] = psum.tile([P, width], F32, name="h2_ps%d_%d" % (t, u), tag=tag)
@@ -216,11 +226,11 @@ def tile_picked_pqmixghopmhopb_none_p_kernel(tc, x_words, x_scales, d_words, d_s
             for first in (0, HALF):
                 product(t, w2_mx, (x2_words, x2_scales), first, first + HALF, True, False)
 
-        held = {128: "larger3_0", 256: "larger3_1", 384: "h3"}
+        held = {0: "members2_1", 128: "larger3_0", 256: "larger3_1", 384: "h3"}
         st_n2 = {}
         for first, last in Z_CHUNKS:
             st_n2[first] = keep.tile(
-                [P, PACK, last - first], F32, align_bytes=64, name="st_n2_%d" % first, tag=held.get(first, "st_n2")
+                [P, PACK, last - first], F32, align_bytes=64, name="st_n2_%d" % first, tag=held[first]
             )
             for t in range(PACK):
                 gather("vector" if (first, t) in {(0, 2), (0, 3), (128, 3)} else "scalar", st_n2[first][:, t, :], st[:, t, :], entries(n2_t, first, last))
@@ -245,7 +255,7 @@ def tile_picked_pqmixghopmhopb_none_p_kernel(tc, x_words, x_scales, d_words, d_s
             for t in range(2):
                 product(t, w1_mx, (z_codes, z_scales), first, last, False, last % HALF == 0)
 
-        w1_mx.append(quantize("w1_late", round_weights("scalar", w1_raw, 1, "st_n2"), HALF))
+        w1_mx.append(quantize("w1_late", round_weights("scalar", w1_raw, 1, "members2_1"), HALF))
         w2_mx.append(quantize("w2_late", round_weights("scalar", w2_raw, 1, "larger3_0"), HALF))
         for t in range(2, PACK):
             product(t, w1_mx, (z_codes, z_scales), 0, S, True, False)
@@ -274,10 +284,10 @@ def tile_picked_pqmixghopmhopb_none_p_kernel(tc, x_words, x_scales, d_words, d_s
                 cols = slice(HALF * u, HALF * (u + 1))
                 result = keep.tile([P, HALF], F32, name="result%d_%d" % (t, u))
                 offsets = entries(n4_t, cols.start, cols.stop)
-                if (t, u) in {(1, 1), (2, 1), (3, 0), (3, 1)}:
+                if (t, u) in {(1, 1), (2, 1), (3, 0), (3, 1)} | set():
                     st2_n4 = keep.tile([P, HALF], F32, name="st2_n4_%d_%d" % (t, u))
-                    gather("scalar", st2_n4[:], st2[:], offsets)
-                    nc.vector.tensor_tensor(result[:], st2_n4[:], half_h2[:, cols], ALU.subtract)
+                    gather("vector" if (t, u) in set() else "scalar", st2_n4[:], st2[:], offsets)
+                    (nc.gpsimd if (t, u) in set() else nc.vector).tensor_tensor(result[:], st2_n4[:], half_h2[:, cols], ALU.subtract)
                 else:
                     nc.vector.tensor_tensor(result[:], st2[:].indirect(offsets), half_h2[:, cols], ALU.subtract)
                 nc.sync.dma_start(out_rows[t][:, cols], result[:])

from contextlib import ExitStack

import concourse.mybir as mybir

K, T, S, N, G, H, W = 512, 1024, 512, 512, 2048, 512, 1024
FLOPS = 3 * 2 * 512 * 512 * 512

F32 = mybir.dt.float32
BF16 = mybir.dt.bfloat16
I32 = mybir.dt.int32
U32 = mybir.dt.uint32
U16 = mybir.dt.uint16
U8 = mybir.dt.uint8
FP8X4 = mybir.dt.float8_e4m3fn_x4
ALU = mybir.AluOpType
ACT = mybir.ActivationFunctionType

P = 128
PACK = 4
LIST_ROWS = 16
SPARE = 16
Z_CHUNKS = ((0, 128), (128, 256), (256, 384), (384, 512))
HALF = S // 2


def entries(list_tile, first, last):
    return list_tile[:, first // LIST_ROWS : last // LIST_ROWS]


def tile_picked_pqmixghopmhopb_none_p_kernel(tc, x_words, x_scales, d_words, d_scales, gn, w1, w2, offs, k1, n1, n2, two, n3, n4, out):
    nc = tc.nc

    with ExitStack() as ctx:
        keep = ctx.enter_context(tc.tile_pool(name="keep", bufs=1))
        psum = ctx.enter_context(tc.psum_pool(name="psum", bufs=1))

        def load_list(name, dram):
            list_tile = keep.tile(list(dram.shape), U16, name=name)
            nc.sync.dma_start(list_tile[:], dram)
            return list_tile

        def gather(engine, dst, window, offsets):
            if engine == "scalar":
                nc.scalar.activation(dst, window.indirect(offsets), ACT.Copy)
            else:
                nc.vector.tensor_copy(dst, window.indirect(offsets))

        d_scale_table = keep.tile([P, G], U8, align_bytes=64, tag="then_w2")
        x_scale_table = keep.tile([P, T], U8, align_bytes=64)
        d_scale_rows = keep.tile([P, H], U8, align_bytes=64, tag="then_x2_words")
        nc.vector.memset(d_scale_table[:].bitcast(I32), 0)
        nc.vector.memset(x_scale_table[:].bitcast(I32), 0)
        nc.vector.memset(d_scale_rows[:].bitcast(I32), 0)

        k1_t = load_list("k1_t", k1)
        offs_t = load_list("offs_t", offs)
        nc.sync.dma_start(d_scale_table[0:P:8, :].bitcast(I32), d_scales[0].bitcast(I32))
        for q, queue in enumerate((nc.scalar, nc.scalar, nc.sync, nc.sync)):
            queue.dma_start(
                x_scale_table[32 * q : 32 * q + 4, :].bitcast(I32), x_scales[0, 4 * q : 4 * q + 4, :].bitcast(I32)
            )
        d_table = keep.tile([P, G], I32, align_bytes=64)
        nc.sync.dma_start(d_table[:], d_words[0].rearrange("p n r -> p (n r)").bitcast(I32))
        x_table = keep.tile([P, T], I32, align_bytes=64)
        nc.sync.dma_start(x_table[:], x_words[0].rearrange("p n r -> p (n r)").bitcast(I32))
        gn_t = keep.tile([P, PACK], F32)
        nc.sync.dma_start(gn_t[:], gn.rearrange("(p t) o -> p (t o)", t=PACK))

        d_scale_picked = keep.tile([P, H], U8, align_bytes=64, tag="then_xq1")
        nc.vector.tensor_copy(d_scale_picked[:], d_scale_table[:].indirect(k1_t[:]))
        for r in range(4):
            nc.sync.dma_start(d_scale_rows[r:P:32, :].bitcast(I32), d_scale_picked[8 * r : P : 32, :].bitcast(I32))
        n1_t = load_list("n1_t", n1)
        two_t = load_list("two_t", two)
        w2_raw = keep.tile([P, PACK, N], F32, align_bytes=64, tag="then_w2")
        nc.sync.dma_start(w2_raw[:], w2.rearrange("(p j) n -> p j n", j=PACK))

        xq_scales = keep.tile([P, S], U8, align_bytes=64, tag="x_picked_scales")
        nc.vector.tensor_copy(xq_scales[:], x_scale_table[:].indirect(offs_t[:]))
        d_picked = []
        for u, tag in enumerate(("then_xq0", "then_w1")):
            words = keep.tile([P, HALF], U32, align_bytes=64, name="d_picked%d" % u, tag=tag)
            nc.vector.tensor_copy(words[:], d_table[:].bitcast(U32).indirect(entries(k1_t, HALF * u, HALF * (u + 1))))
            d_picked.append(words)
        d_dealt = keep.tile([P, PACK, P], U32, align_bytes=64)
        for u in range(2):
            nc.vector.tensor_copy(
                d_dealt[:, :, P // 2 * u : P // 2 * (u + 1)].rearrange("p t m -> p m t"),
                d_picked[u][:].rearrange("p (m t) -> p m t", t=PACK),
            )
        xq_words = []

        def pick_x_words(u):
            words = keep.tile([P, HALF], U32, align_bytes=64, name="xq_words%d" % u, tag="then_xq%d" % u)
            nc.vector.tensor_copy(words[:], x_table[:].bitcast(U32).indirect(entries(offs_t, HALF * u, HALF * (u + 1))))
            xq_words.append(words)

        pick_x_words(0)
        d_scale_dealt = keep.tile([P, H], U8, align_bytes=64)
        nc.vector.tensor_copy(
            d_scale_dealt[:].rearrange("p (t m) -> p t m", t=PACK),
            d_scale_rows[:].rearrange("p (m t) -> p t m", t=PACK),
        )
        pick_x_words(1)
        w1_raw = keep.tile([P, PACK, N], F32, align_bytes=64, tag="then_w1")
        nc.sync.dma_start(w1_raw[:], w1.rearrange("(p j) n -> p j n", j=PACK))

        n2_t = load_list("n2_t", n2)
        n3_t = load_list("n3_t", n3)
        n4_t = load_list("n4_t", n4)

        gain = keep.tile([P, PACK], F32)
        nc.scalar.activation(gain[:], gn_t[:], ACT.Abs, scale=0.0625)
        widest = max(b - a for a, b in Z_CHUNKS)
        signs = keep.tile([P, widest, PACK], BF16, align_bytes=64)
        nc.scalar.activation(signs[:], gn_t[:].unsqueeze(1).to_broadcast([P, widest, PACK]), ACT.Sign)

        h_ps = []
        for t in range(PACK):
            if t < 2:
                banks = [psum.tile([P, HALF], F32, name="h_ps%d_%d" % (t, HALF * u)) for u in range(2)]
                pieces = [(HALF * u, HALF * (u + 1), banks[u]) for u in range(2)]
                halves = [bank[:] for bank in banks]
            else:
                bank = psum.tile([P, S], F32, name="h_ps%d_0" % t)
                pieces = [(0, S, bank)]
                halves = [bank[:, :HALF], bank[:, HALF:]]
            for u in range(2):
                nc.tensor.matmul_mx(
                    out=halves[u],
                    lhsT=d_dealt[:, t, :].bitcast(FP8X4),
                    lhsT_scale=d_scale_dealt[:, P * t : P * (t + 1)],
                    rhs=xq_words[u][:].bitcast(FP8X4),
                    rhs_scale=xq_scales[:, HALF * u : HALF * (u + 1)],
                    start=True,
                    stop=True,
                )
            h_ps.append(pieces)

        def round_weights(engine, raw, pair, tag):
            grouped = keep.tile([P, 2, P, PACK], BF16, align_bytes=64, name="grouped_%s%d" % (tag, pair), tag=tag)
            dst = grouped[:].rearrange("p t m j -> p m j t")
            src = raw[:].rearrange("p j (m t) -> p m j t", t=PACK)[:, :, :, 2 * pair : 2 * pair + 2]
            if engine == "scalar":
                nc.scalar.copy(dst, src)
            else:
                nc.vector.tensor_copy(dst, src)
            return grouped[:].rearrange("p t m j -> p (t m j)")

        def quantize(name, grouped, width):
            codes = keep.tile([P, width], U32, align_bytes=64, name=name + "_codes")
            scales = keep.tile([P, width], U8, align_bytes=64, name=name + "_scales")
            nc.vector.quantize_mx(out=codes[:].bitcast(FP8X4), scales=scales[:], in_=grouped)
            return codes, scales

        st = keep.tile([P, PACK, S], F32, align_bytes=64)
        h_tiles = {}

        def leave_psum(t):
            h = keep.tile([P, S + SPARE], F32, align_bytes=64, name="h%d" % t)
            nc.vector.memset(h[:, S:], 0.0)
            for first, last, bank in h_ps[t]:
                nc.scalar.activation(h[:, first:last], bank[:], ACT.Copy, scale=gain[:, t : t + 1])
            h_tiles[t] = h

        def less_larger_member(t, u):
            h = h_tiles[t]
            halves = (0, 1) if t < 2 else (u,)
            width = HALF * len(halves)
            members = keep.tile([P, width, 2], F32, align_bytes=64, name="members%d_%d" % (t, u))
            for v in halves:
                gather(
                    "vector" if t < 2 and v == 1 else "scalar",
                    members[:, HALF * (v - u) : HALF * (v - u + 1), :].rearrange("p j e -> p (j e)"),
                    h[:],
                    entries(n1_t, S * v, S * (v + 1)),
                )
            larger = keep.tile([P, width], F32, align_bytes=64, name="larger%d_%d" % (t, u))
            nc.vector.tensor_tensor(larger[:], members[:, :, 0], members[:, :, 1], ALU.max)
            cols = slice(HALF * u, HALF * u + width)
            nc.vector.tensor_tensor(st[:, t, cols], h[:, cols], larger[:], ALU.subtract)

        x2_words = keep.tile([P, S], U32, align_bytes=64, tag="then_x2_words")
        nc.vector.tensor_copy(x2_words[:], x_table[:].bitcast(U32).indirect(two_t[:]))
        leave_psum(0)
        less_larger_member(0, 0)
        x2_scales = keep.tile([P, S], U8, align_bytes=64, tag="x_picked_scales")
        nc.vector.tensor_copy(x2_scales[:], x_scale_table[:].indirect(two_t[:]))
        leave_psum(1)
        less_larger_member(1, 0)
        w2_early = round_weights("vector", w2_raw, 0, "w2_early")
        leave_psum(2)
        less_larger_member(2, 0)
        w2_mx = [quantize("w2_early", w2_early, HALF)]
        w1_early = round_weights("vector", w1_raw, 0, "w1_early")
        less_larger_member(2, 1)
        leave_psum(3)
        less_larger_member(3, 0)
        w1_mx = [quantize("w1_early", w1_early, HALF)]
        less_larger_member(3, 1)

        h2_ps = {}
        for t, tags in enumerate((("h_ps0_0", "h_ps0_256"), ("h_ps1_0", "h_ps1_256"), ("h2_ps2",), ("h2_ps3",))):
            width = S // len(tags)
            for u, tag in enumerate(tags):
                h2_ps[t, width * u] = psum.tile([P, width], F32, name="h2_ps%d_%d" % (t, u), tag=tag)

        def h2_view(t, first, last):
            base = first // HALF * HALF if t < 2 else 0
            return h2_ps[t, base][:, first - base : last - base]

        def product(t, weights, moving, first, last, start, stop):
            codes, scales = weights[t // 2]
            cols = slice(P * (t % 2), P * (t % 2 + 1))
            nc.tensor.matmul_mx(
                out=h2_view(t, first, last),
                lhsT=codes[:, cols].bitcast(FP8X4),
                lhsT_scale=scales[:, cols],
                rhs=moving[0][:, first:last].bitcast(FP8X4),
                rhs_scale=moving[1][:, first:last],
                start=start,
                stop=stop,
            )

        for t in range(2):
            for first in (0, HALF):
                product(t, w2_mx, (x2_words, x2_scales), first, first + HALF, True, False)

        held = {0: "members2_1", 128: "larger3_0", 256: "larger3_1", 384: "h3"}
        st_n2 = {}
        for first, last in Z_CHUNKS:
            st_n2[first] = keep.tile(
                [P, PACK, last - first], F32, align_bytes=64, name="st_n2_%d" % first, tag=held[first]
            )
            for t in range(PACK):
                gather("vector" if (first, t) in {(0, 2), (0, 3), (128, 3)} else "scalar", st_n2[first][:, t, :], st[:, t, :], entries(n2_t, first, last))
        z_codes = keep.tile([P, S], U32, align_bytes=64)
        z_scales = keep.tile([P, S], U8, align_bytes=64)
        for first, last in Z_CHUNKS:
            width = last - first
            z_abs = keep.tile([P, width, PACK], BF16, align_bytes=64, name="z_abs%d" % first, tag="z_abs", bufs=2)
            nc.vector.tensor_tensor(
                z_abs[:].rearrange("p (c i) t -> p c t i", i=4),
                st[:, :, first:last].rearrange("p t (c i) -> p c t i", i=4),
                st_n2[first][:].rearrange("p t (c i) -> p c t i", i=4),
                ALU.max,
            )
            z = keep.tile([P, width, PACK], BF16, align_bytes=64, name="z%d" % first)
            nc.vector.tensor_tensor(z[:], z_abs[:], signs[:, :width, :], ALU.mult)
            nc.vector.quantize_mx(
                out=z_codes[:, first:last].bitcast(FP8X4),
                scales=z_scales[:, first:last],
                in_=z[:].rearrange("p j t -> p (j t)"),
            )
            for t in range(2):
                product(t, w1_mx, (z_codes, z_scales), first, last, False, last % HALF == 0)

        w1_mx.append(quantize("w1_late", round_weights("scalar", w1_raw, 1, "members2_1"), HALF))
        w2_mx.append(quantize("w2_late", round_weights("scalar", w2_raw, 1, "larger3_0"), HALF))
        for t in range(2, PACK):
            product(t, w1_mx, (z_codes, z_scales), 0, S, True, False)
            product(t, w2_mx, (x2_words, x2_scales), 0, S, False, True)

        out_rows = out.rearrange("(p t) j -> t p j", t=PACK)
        half_h2s, st2s = [], []
        for t in range(PACK):
            half_h2 = keep.tile([P, S], F32, name="half_h2_%d" % t)
            for first, last in ((0, HALF), (HALF, S)) if t < 2 else ((0, S),):
                if (t, first) in {(1, 256)}:
                    nc.vector.tensor_scalar(half_h2[:, first:last], h2_view(t, first, last), 0.5, None, ALU.mult)
                else:
                    nc.scalar.activation(half_h2[:, first:last], h2_view(t, first, last), ACT.Copy, scale=0.5)
            st2 = keep.tile([P, S], F32, name="st2_%d" % t)
            for u in range(2):
                cols = slice(HALF * u, HALF * (u + 1))
                half_n3 = keep.tile([P, HALF], F32, name="half_n3_%d_%d" % (t, u))
                gather("vector" if (t, u) in {(0, 1), (1, 1)} else "scalar", half_n3[:], half_h2[:], entries(n3_t, cols.start, cols.stop))
                nc.vector.scalar_tensor_tensor(st2[:, cols], half_n3[:], 2.0, h2_view(t, cols.start, cols.stop), ALU.mult, ALU.max)
            half_h2s.append(half_h2)
            st2s.append(st2)
        for t in range(PACK):
            half_h2, st2 = half_h2s[t], st2s[t]
            for u in range(2):
                cols = slice(HALF * u, HALF * (u + 1))
                result = keep.tile([P, HALF], F32, name="result%d_%d" % (t, u))
                offsets = entries(n4_t, cols.start, cols.stop)
                if (t, u) in {(1, 1), (2, 1), (3, 0), (3, 1)} | set():
                    st2_n4 = keep.tile([P, HALF], F32, name="st2_n4_%d_%d" % (t, u))
                    gather("vector" if (t, u) in set() else "scalar", st2_n4[:], st2[:], offsets)
                    (nc.gpsimd if (t, u) in set() else nc.vector).tensor_tensor(result[:], st2_n4[:], half_h2[:, cols], ALU.subtract)
                else:
                    nc.vector.tensor_tensor(result[:], st2[:].indirect(offsets), half_h2[:, cols], ALU.subtract)
                nc.sync.dma_start(out_rows[t][:, cols], result[:])
